import numpy as np
import ml_dtypes


def mxq(x, axis, fmt="e4m3"):
    dtype, down = {"e4m3": (ml_dtypes.float8_e4m3fn, 7), "e5m2": (ml_dtypes.float8_e5m2, 14)}[fmt]
    v = np.moveaxis(np.asarray(x, np.float32).astype(ml_dtypes.bfloat16).astype(np.float64), axis, -1)
    blocks = v.reshape(v.shape[:-1] + (-1, 32))
    amax = np.abs(blocks).max(-1, keepdims=True)
    byte = np.maximum(np.where(amax > 0, np.frexp(amax)[1] - 1 + 127, 0) - down, 1)
    scale = np.exp2(byte - 127.0)
    codes = (blocks / scale).astype(np.float32).astype(dtype).astype(np.float64)
    return np.moveaxis((codes * scale).reshape(v.shape), -1, axis)


WIDE = False


def mx_kscale(k):
    if not WIDE:
        return np.ones(k)
    levels = np.array([10, -10, 5, -5, 0])
    if k % 512:
        return np.exp2(np.random.permutation(np.resize(levels, k // 32))).repeat(32)
    a = np.empty((k // 512, 16))
    for p in range(k // 512):
        a[p, :8] = np.random.permutation(np.resize(levels, 8))
        for g in range(8):
            far = levels[np.abs(levels - a[p, g]) >= 10]
            a[p, g + 8] = far[np.random.randint(len(far))]
    return np.exp2(a.ravel()).repeat(32)


def f64(x):
    return np.asarray(x).astype(np.float64)


def striped(idx):
    return np.tile(np.asarray(idx).reshape(-1, 16).T, (8, 1)).astype(np.uint16)


def unstriped(offs):
    return offs[:16].T.reshape(-1).astype(np.int64)


E2M1 = np.array([0.0, 0.5, 1.0, 1.5, 2.0, 3.0, 4.0, 6.0, -0.0, -0.5, -1.0, -1.5, -2.0, -3.0, -4.0, -6.0])


def pack_weight(w, fmt):
    k, n = w.shape
    w = f64(np.asarray(w, np.float32).astype(ml_dtypes.bfloat16)).reshape(k // 32, 32, n)
    amax = np.abs(w).max(1)
    if fmt == "e4m3":
        byte = np.frexp(amax)[1] - 1 + 127 - 7
    else:
        mant, ex = np.frexp(amax / 6.0)
        byte = np.where(mant > 0.5, ex, ex - 1) + 127
    byte = np.clip(np.where(amax > 0, byte, 1), 1, 254)
    scaled = (w * np.exp2(127.0 - byte)[:, None, :]).reshape(k, n).astype(np.float32)
    by_word = np.ascontiguousarray(scaled.reshape(k // 512, 128, 4, n).transpose(0, 1, 3, 2))
    if fmt == "e4m3":
        words = by_word.astype(ml_dtypes.float8_e4m3fn).view(np.uint8)
    else:
        c = by_word.astype(ml_dtypes.float4_e2m1fn).view(np.uint8) & 0xF
        words = (c[..., 0::2] | (c[..., 1::2] << 4)).reshape(k // 512, 128, 2 * n)
    return np.ascontiguousarray(words), np.ascontiguousarray(byte.astype(np.uint8).reshape(k // 512, 16, n))


def unpack_weight(words, scales, fmt):
    g, _, n = scales.shape
    words = np.ascontiguousarray(words).reshape(g, 128, n, -1)
    if fmt == "e4m3":
        vals = words.view(ml_dtypes.float8_e4m3fn).astype(np.float64)
    else:
        nib = np.empty((g, 128, n, 4), np.uint8)
        nib[..., 0::2] = words & 0xF
        nib[..., 1::2] = words >> 4
        vals = E2M1[nib]
    vals = vals * np.repeat(np.exp2(scales.astype(np.float64) - 127.0), 8, axis=1)[..., None]
    return vals.transpose(0, 1, 3, 2).reshape(g * 512, n)


def e4m3fn_bytes(y):
    return np.clip(np.asarray(y, np.float64), -448.0, 448.0).astype(np.float32).astype(ml_dtypes.float8_e4m3fn).view(np.uint8)


def e4m3fn_values(b):
    return np.asarray(b, np.uint8).view(ml_dtypes.float8_e4m3fn).astype(np.float64)


K, V, J, N = 512, 1024, 256, 256


def setup_inputs():
    n = np.random.standard_normal
    idx = np.random.permutation(V)[:J]
    fk = mx_kscale(K)
    wp = pack_weight(n((K, N)) * 1 / np.sqrt(K) / fk[:, None], "e4m3")
    w2p = pack_weight(n((K, N)) * 1 / np.sqrt(K) / fk[:, None], "e2m1")
    return {
        "ca": e4m3fn_bytes(60.0 * n((K, V))),
        "sa": (np.random.uniform(0.004, 0.012, (K, 1)) * fk[:, None]).astype(np.float32),
        "sb": (np.random.uniform(0.004, 0.012, (K, 1)) * fk[:, None]).astype(np.float32),
        "w_words": wp[0],
        "w_scales": wp[1],
        "w2_words": w2p[0],
        "w2_scales": w2p[1],
        "offs": striped(idx),
    }


def reference(ca, sa, sb, w_words, w_scales, w2_words, w2_scales, offs):
    idx = unstriped(offs)
    wu = unpack_weight(w_words, w_scales, "e4m3")
    w2u = unpack_weight(w2_words, w2_scales, "e2m1")
    z1 = np.maximum(e4m3fn_values(ca)[:, idx], 0.0) * f64(sa)
    z2 = np.maximum(-e4m3fn_values(ca)[:, idx], 0.0) * f64(sb)
    z1q = mxq(z1, 0, "e4m3")
    z2q = mxq(z2, 0, "e4m3")
    p = wu.T @ z1q + w2u.T @ z2q
    return p

from contextlib import ExitStack

import concourse.mybir as mybir

K, V, J, N = 512, 1024, 256, 256
FLOPS = 2 * 2 * K * N * J

F32 = mybir.dt.float32
BF16 = mybir.dt.bfloat16
I32 = mybir.dt.int32
U32 = mybir.dt.uint32
U16 = mybir.dt.uint16
U8 = mybir.dt.uint8
E4M3 = mybir.dt.float8_e4m3fn
E4M3_X4 = mybir.dt.float8_e4m3fn_x4
E2M1_X4 = mybir.dt.float4_e2m1fn_x4
ALU = mybir.AluOpType

P = 128
PACK = 4
HALF = J // 2
RUN = 4


def tile_list_signedhalves_kernel(tc, ca, sa, sb, w_words, w_scales, w2_words, w2_scales, offs, out):
    nc = tc.nc
    with ExitStack() as ctx:
        keep = ctx.enter_context(tc.tile_pool(name="keep", bufs=1))
        psum = ctx.enter_context(tc.psum_pool(name="psum", bufs=1))

        offsets = keep.tile([P, J // 16], U16, name="offsets")
        nc.sync.dma_start(offsets[:], offs)
        rows = ca.rearrange("(p t) v -> p t v", t=PACK)
        table = []
        for t in range(PACK):
            rows_t = keep.tile([P, V], U8, name=f"table{t}")
            nc.sync.dma_start(rows_t[:], rows[:, t, :])
            table.append(rows_t)

        rise = keep.tile([P, PACK], F32, name="rise")
        fall = keep.tile([P, PACK], F32, name="fall")
        staged = keep.tile([4, 4, N], U8, name="staged")
        nc.scalar.dma_start(staged[:].bitcast(I32), w_scales[0].rearrange("(q r) n -> r q n", r=4).bitcast(I32))
        nc.scalar.dma_start(fall[:], sb.rearrange("(p t) o -> p (t o)", t=PACK))
        nc.scalar.dma_start(rise[:], sa.rearrange("(p t) o -> p (t o)", t=PACK))
        neg_fall = keep.tile([P, PACK], F32, name="neg_fall")
        nc.vector.tensor_scalar(neg_fall[:], fall[:], -1.0, None, ALU.mult)

        w_codes = keep.tile([P, N], U32, name="w_codes", align_bytes=64)
        w2_codes = keep.tile([P, 2 * N], U8, name="w2_codes", align_bytes=64)
        w_plane = keep.tile([P, N], U8, name="w_plane", align_bytes=64)
        w2_plane = keep.tile([P, N], U8, name="w2_plane", align_bytes=64)
        nc.sync.dma_start(w_codes[:].bitcast(I32), w_words[0].rearrange("p n t -> p (n t)").bitcast(I32))
        nc.sync.dma_start(w2_codes[:].bitcast(I32), w2_words[0].bitcast(I32))
        nc.vector.memset(w_plane[:].bitcast(U32), 0)
        nc.vector.memset(w2_plane[:].bitcast(U32), 0)
        for q in range(4):
            live = slice(32 * q, 32 * q + 4)
            nc.vector.tensor_copy(w_plane[live, :].bitcast(I32), staged[:, q, :].bitcast(I32))
            nc.sync.dma_start(w2_plane[live, :].bitcast(I32), w2_scales[0][4 * q : 4 * q + 4, :].bitcast(I32))

        levels = {}
        planes = {}
        woven = {}
        codes = {}
        zscale = {}
        for h in range(2):
            for s in range(2):
                planes[h, s] = keep.tile([P, PACK, HALF], BF16, name=f"planes{h}{s}")
                woven[h, s] = keep.tile([P, HALF, PACK], BF16, name=f"woven{h}{s}", align_bytes=64)
                codes[h, s] = keep.tile([P, HALF], U32, name=f"codes{h}{s}", align_bytes=64)
                zscale[h, s] = keep.tile([P, HALF], U8, name=f"zscale{h}{s}", align_bytes=64)

        def look_up(h):
            tag = "reused" if h == 1 else "picked0"
            picked = keep.tile([P, PACK, HALF], U8, name=f"picked{h}", tag=tag)
            cols = slice(h * HALF // 16, (h + 1) * HALF // 16)
            for t in range(PACK):
                nc.vector.tensor_copy(picked[:, t, :], table[t][:].indirect(offsets[:, cols]))
                tag = "reused" if (h, t) == (0, 2) else f"levels{h}{t}"
                levels[h, t] = keep.tile([P, HALF], F32, name=f"levels{h}{t}", tag=tag)
                nc.scalar.copy(levels[h, t][:], picked[:, t, :].bitcast(E4M3))

        def signed_parts(h, t):
            for s in ((0, 1) if h == 0 else (1, 0)):
                step, clip = ((rise, ALU.max), (neg_fall, ALU.min))[s]
                nc.vector.tensor_scalar(planes[h, s][:, t, :], levels[h, t][:], 0.0, step[:, t : t + 1], clip, ALU.mult)

        def weave(h, s, copy):
            copy(
                woven[h, s][:].rearrange("p (c i) t -> p c t i", i=RUN),
                planes[h, s][:].rearrange("p t (c i) -> p c t i", i=RUN),
            )

        def quantise(h, s):
            nc.vector.quantize_mx(
                out=codes[h, s][:].bitcast(E4M3_X4),
                scales=zscale[h, s][:],
                in_=woven[h, s][:].rearrange("p j t -> p (j t)"),
            )

        def product(acc, h, a, s, first):
            cols = slice(a * P, (a + 1) * P)
            if s == 0:
                weights, plane = w_codes[:, cols].bitcast(E4M3_X4), w_plane
            else:
                weights, plane = w2_codes[:, 2 * a * P : 2 * (a + 1) * P].bitcast(E2M1_X4), w2_plane
            nc.tensor.matmul_mx(
                out=acc, lhsT=weights, lhsT_scale=plane[:, cols],
                rhs=codes[h, s][:].bitcast(E4M3_X4), rhs_scale=zscale[h, s][:],
                start=first, stop=not first,
            )

        out_rows = out.rearrange("(a p) j -> p a j", a=2)

        look_up(0)
        for t in range(PACK):
            signed_parts(0, t)
        look_up(1)
        weave(0, 0, nc.scalar.copy)
        weave(0, 1, nc.scalar.copy)
        for t in range(PACK):
            signed_parts(1, t)
        quantise(0, 0)
        weave(1, 0, nc.vector.tensor_copy)
        weave(1, 1, nc.scalar.copy)
        quantise(0, 1)
        quantise(1, 0)
        quantise(1, 1)

        for h in range(2):
            acc = [psum.tile([P, HALF], F32, name=f"acc{h}{a}") for a in range(2)]
            order = (0, 1)
            for s in order:
                for a in range(2):
                    product(acc[a][:], h, a, s, s == order[0])
            cols = slice(h * HALF, (h + 1) * HALF)
            if h == 0:
                result = keep.tile([P, 2, HALF], F32, name="result0")
                for a in range(2):
                    nc.scalar.copy(result[:, a, :], acc[a][:])
                nc.sync.dma_start(out_rows[:, :, cols], result[:])
            else:
                for a, copy, queue in ((0, nc.vector.tensor_copy, nc.sync), (1, nc.scalar.copy, nc.scalar)):
                    result = keep.tile([P, HALF], F32, name=f"result1{a}")
                    copy(result[:], acc[a][:])
                    queue.dma_start(out_rows[:, a, cols], result[:])
